import numpy as np
import ml_dtypes


def mxq(x, axis, fmt="e4m3"):
    dtype, down = {"e4m3": (ml_dtypes.float8_e4m3fn, 7), "e5m2": (ml_dtypes.float8_e5m2, 14)}[fmt]
    v = np.moveaxis(np.asarray(x, np.float32).astype(ml_dtypes.bfloat16).astype(np.float64), axis, -1)
    blocks = v.reshape(v.shape[:-1] + (-1, 32))
    amax = np.abs(blocks).max(-1, keepdims=True)
    byte = np.maximum(np.where(amax > 0, np.frexp(amax)[1] - 1 + 127, 0) - down, 1)
    scale = np.exp2(byte - 127.0)
    codes = (blocks / scale).astype(np.float32).astype(dtype).astype(np.float64)
    return np.moveaxis((codes * scale).reshape(v.shape), -1, axis)


WIDE = False


def mx_kscale(k):
    if not WIDE:
        return np.ones(k)
    levels = np.array([10, -10, 5, -5, 0])
    if k % 512:
        return np.exp2(np.random.permutation(np.resize(levels, k // 32))).repeat(32)
    a = np.empty((k // 512, 16))
    for p in range(k // 512):
        a[p, :8] = np.random.permutation(np.resize(levels, 8))
        for g in range(8):
            far = levels[np.abs(levels - a[p, g]) >= 10]
            a[p, g + 8] = far[np.random.randint(len(far))]
    return np.exp2(a.ravel()).repeat(32)


def f64(x):
    return np.asarray(x).astype(np.float64)


def striped(idx):
    return np.tile(idx.reshape(-1, 16).T, (8, 1)).astype(np.uint16)


def unstriped(offs):
    return offs[:16].T.reshape(-1).astype(np.int64)


def striped8(idx):
    return np.concatenate([x.reshape(-1, 16).T for x in idx]).astype(np.uint16)


def runs(offs, k):
    lists = np.stack([offs[16 * r : 16 * r + 16].T.reshape(-1) for r in range(8)]).astype(np.int64)
    return lists[np.arange(k) % 512 // 64]


def pack_weight(w):
    k, n = w.shape
    w = f64(np.asarray(w, np.float32).astype(ml_dtypes.bfloat16)).reshape(k // 32, 32, n)
    amax = np.abs(w).max(1)
    byte = np.clip(np.where(amax > 0, np.frexp(amax)[1] - 1 + 127 - 7, 1), 1, 254)
    scaled = (w * np.exp2(127.0 - byte)[:, None, :]).reshape(k, n).astype(np.float32)
    words = np.ascontiguousarray(scaled.reshape(k // 512, 128, 4, n).transpose(0, 1, 3, 2)).astype(ml_dtypes.float8_e4m3fn).view(np.uint8)
    return words, np.ascontiguousarray(byte.astype(np.uint8).reshape(k // 512, 16, n))


def unpack_weight(words, scales):
    g, p, n, _ = words.shape
    vals = np.ascontiguousarray(words).view(ml_dtypes.float8_e4m3fn).astype(np.float64) * np.repeat(np.exp2(scales.astype(np.float64) - 127.0), 8, axis=1)[..., None]
    return vals.transpose(0, 1, 3, 2).reshape(g * 512, n)


K, T, S, N, H = 512, 2048, 512, 512, 512


def setup_inputs():
    n = np.random.standard_normal
    s = mx_kscale(K)[:, None]
    u = mx_kscale(S)
    packed_xT = pack_weight(n((K, T)) * s)
    return {
        "x_words": packed_xT[0],
        "x_scales": packed_xT[1],
        "wa": (n((K, H)) / np.sqrt(K) / s).astype(np.float32),
        "gt": (np.random.uniform(0.5, 1.5, (S, 1)) * u[:, None]).astype(np.float32),
        "w1": (n((S, N)) / np.sqrt(S) / u[:, None]).astype(np.float32),
        "offs": striped(np.random.permutation(T)[:S]),
        "n1": striped8(np.stack([np.random.permutation(H) for _ in range(8)])),
        "n2": striped8(np.stack([np.random.permutation(H) for _ in range(8)])),
        "n3": striped8(np.stack([np.random.permutation(H) for _ in range(8)])),
    }


def reference(x_words, x_scales, wa, gt, w1, offs, n1, n2, n3):
    xq = unpack_weight(x_words, x_scales)[:, unstriped(offs)]
    y = xq.T @ mxq(f64(wa), 0, "e4m3")
    pa = y[np.arange(S)[:, None], runs(n1, S)]
    pb = y[np.arange(S)[:, None], runs(n2, S)]
    mu = 0.3125 * (y + pa + pb)
    z = f64(gt) * ((y - mu) / (np.sqrt((pa - mu) ** 2 + (pb - mu) ** 2 + 0.25)))
    h = mxq(f64(w1), 0, "e4m3").T @ mxq(z, 0, "e4m3")
    st = h - (h[np.arange(N)[:, None], runs(n3, N)])
    return st - (0.5 * (st[np.arange(N)[:, None], runs(n3, N)]))

@@ -1,0 +1,280 @@
+from contextlib import ExitStack
+
+import concourse.mybir as mybir
+from concourse.masks import make_identity
+
+F32 = mybir.dt.float32
+BF16 = mybir.dt.bfloat16
+I32 = mybir.dt.int32
+U32 = mybir.dt.uint32
+U16 = mybir.dt.uint16
+U8 = mybir.dt.uint8
+FP8X4 = mybir.dt.float8_e4m3fn_x4
+ALU = mybir.AluOpType
+ACT = mybir.ActivationFunctionType
+
+P = 128
+K, T, S, N, H = 512, 2048, 512, 512, 512
+FLOPS = 2 * S * K * H + 2 * N * S * H
+C = 0.3125
+UNITS = [(0, 256, 0), (0, 256, 1), (256, 384, 0), (256, 384, 1), (384, 512, 0), (384, 512, 1)]
+HALF = 256
+WA_PARTS = [(0, 256), (256, 384), (384, 512)]
+
+
+def tile_picked_tokstdtwice_none_p_kernel(
+    tc, x_words, x_scales, wa, gt, w1, offs, n1, n2, n3, out
+):
+    nc = tc.nc
+    with ExitStack() as ctx:
+        keep = ctx.enter_context(tc.tile_pool(name="keep", bufs=1))
+        work = ctx.enter_context(tc.tile_pool(name="work", bufs=3))
+        psum = ctx.enter_context(tc.psum_pool(name="psum", bufs=1))
+
+        def list_tile(name):
+            return keep.tile([P, 32], U16, name=name)
+
+        offs_t, n1_t, n2_t, n3_t = (list_tile(nm) for nm in ("offs_t", "n1_t", "n2_t", "n3_t"))
+        gt_t = keep.tile([P, 4], F32, name="gt_t")
+        xw = keep.tile([P, T], U32, name="xw", align_bytes=64)
+        xs = keep.tile([P, T], U8, name="xs", align_bytes=64)
+        wa_raw = [keep.tile([P, 4, c1 - c0], F32, name="wa_raw%d" % c0) for c0, c1 in WA_PARTS]
+        w1_raw = [keep.tile([P, 4, HALF], F32, name="w1_raw%d" % i) for i in range(2)]
+        ident = keep.tile([P, P], F32, name="ident")
+
+        nc.vector.memset(xs[:].bitcast(I32), 0)
+        make_identity(nc, ident[:])
+        xs_in = keep.tile([P, T], U8, name="xs_in", align_bytes=64)
+        for q in range(4):
+            nc.sync.dma_start(xs_in[32 * q : 32 * q + 4, :].bitcast(I32), x_scales[0, 4 * q : 4 * q + 4, :].bitcast(I32))
+        nc.sync.dma_start(offs_t[:], offs)
+        nc.sync.dma_start(gt_t[:], gt.rearrange("(p t) o -> p (t o)", t=4))
+        nc.sync.dma_start(xw[:].bitcast(I32), x_words[0].rearrange("p n r -> p (n r)").bitcast(I32))
+        wa_v = wa.rearrange("(p j) c -> p j c", j=4)
+        for i, (c0, c1) in enumerate(WA_PARTS):
+            nc.sync.dma_start(wa_raw[i][:], wa_v[:, :, c0:c1])
+        nc.sync.dma_start(n1_t[:], n1)
+        nc.sync.dma_start(n2_t[:], n2)
+        w1_v = w1.rearrange("(p j) c -> p j c", j=4)
+        for i in range(2):
+            nc.sync.dma_start(w1_raw[i][:], w1_v[:, :, i * HALF : (i + 1) * HALF])
+        nc.sync.dma_start(n3_t[:], n3)
+
+        for q in range(4):
+            rows = slice(32 * q, 32 * q + 4)
+            nc.vector.tensor_copy(xs[rows, :].bitcast(I32), xs_in[rows, :].bitcast(I32))
+        gw = keep.tile([P, 4], F32, name="gw")
+        gk = keep.tile([P, 4], F32, name="gk")
+        gsafe = keep.tile([P, 4], F32, name="gsafe")
+        s_d = keep.tile([P, 4], F32, name="s_d")
+        s_e = keep.tile([P, 4], F32, name="s_e")
+        nc.vector.tensor_scalar(gw[:], gt_t[:], -C, None, ALU.mult)
+        nc.vector.tensor_scalar(gk[:], gt_t[:], 1.0 - C, None, ALU.mult)
+        nc.vector.scalar_tensor_tensor(gsafe[:], gw[:], 0.0, gw[:], ALU.is_equal, ALU.add)
+        nc.vector.reciprocal(s_d[:], gsafe[:])
+        nc.vector.tensor_scalar(s_e[:], s_d[:], 0.375 / 1.32, None, ALU.mult)
+
+        xg_w = keep.tile([P, S], U32, name="xg_w", align_bytes=64)
+        xg_s = keep.tile([P, S], U8, name="xg_s", align_bytes=64)
+        xd_w = keep.tile([P, S], U32, name="xd_w", align_bytes=64)
+        xd_s = keep.tile([P, S], U8, name="xd_s", align_bytes=64)
+        nc.vector.tensor_copy(xg_s[:], xs[:].indirect(offs_t[:]))
+        nc.vector.tensor_copy(xg_w[:], xw[:].indirect(offs_t[:]))
+        nc.vector.tensor_copy(xd_s[:].rearrange("p (t m) -> p t m", t=4), xg_s[:].rearrange("p (m t) -> p t m", t=4))
+        nc.vector.tensor_copy(xd_w[:].rearrange("p (t m) -> p t m", t=4), xg_w[:].rearrange("p (m t) -> p t m", t=4))
+
+        wa_c, wa_s = [], []
+        for i, (c0, c1) in enumerate(WA_PARTS):
+            grouped = keep.tile([P, c1 - c0, 4], BF16, name="wa_bf%d" % i, align_bytes=64)
+            if i == 0:
+                nc.scalar.copy(grouped[:], wa_raw[i][:].rearrange("p j c -> p c j"))
+            else:
+                nc.vector.tensor_copy(grouped[:], wa_raw[i][:].rearrange("p j c -> p c j"))
+            codes = keep.tile([P, c1 - c0], U32, name="wa_c%d" % i, align_bytes=64)
+            scales = keep.tile([P, c1 - c0], U8, name="wa_s%d" % i, align_bytes=64)
+            nc.vector.quantize_mx(codes[:].bitcast(FP8X4), scales[:], grouped[:].rearrange("p c j -> p (c j)"))
+            wa_c.append(codes)
+            wa_s.append(scales)
+
+        y_ps = [psum.tile([P, H], F32, name="y%d" % t, tag="big%d" % t) for t in range(4)]
+        for t in range(4):
+            for i, (c0, c1) in enumerate(WA_PARTS):
+                nc.tensor.matmul_mx(
+                    y_ps[t][:, c0:c1],
+                    lhsT=xd_w[:, t * P : (t + 1) * P].bitcast(FP8X4),
+                    lhsT_scale=xd_s[:, t * P : (t + 1) * P],
+                    rhs=wa_c[i][:].bitcast(FP8X4),
+                    rhs_scale=wa_s[i][:],
+                    start=True,
+                    stop=True,
+                )
+        win = [keep.tile([P, H], F32, name="win%d" % t) for t in range(4)]
+        kk = keep.tile([P, 4, H], F32, name="kk")
+        for u in range(2):
+            for t in (2 * u, 2 * u + 1):
+                nc.scalar.activation(win[t][:], y_ps[t][:], ACT.Copy, scale=gw[:, t : t + 1])
+            for t in (2 * u, 2 * u + 1):
+                nc.scalar.activation(kk[:, t, :], y_ps[t][:], ACT.Copy, scale=gk[:, t : t + 1])
+
+        w1_bf = keep.tile([P, 4, P, 4], BF16, name="w1_bf", align_bytes=64)
+        w1_s = keep.tile([P, N], U8, name="w1_s", align_bytes=64)
+
+        for i in range(2):
+            nc.vector.tensor_copy(
+                w1_bf[:, :, 64 * i : 64 * i + 64, :].rearrange("p t m j -> p m t j"),
+                w1_raw[i][:].rearrange("p j (m t) -> p m t j", t=4),
+            )
+
+        h_ps = [psum.tile([P, H], F32, name="h%d" % t, tag="big%d" % t) for t in range(4)]
+
+        units = UNITS
+        pa, sm, d_ps, r_t, back, z_i = {}, {}, {}, {}, {}, {}
+
+        def gather_first(n):
+            c0, c1, u = units[n]
+            pa[n] = work.tile([P, 2, c1 - c0], F32, name="pa", bufs=1, align_bytes=64)
+            for e in range(2):
+                nc.vector.tensor_copy(pa[n][:, e, :], win[2 * u + e][:].indirect(n1_t[:, c0 // 16 : c1 // 16]))
+
+        def gather_second(n):
+            c0, c1, u = units[n]
+            sm[n] = work.tile([P, 2, c1 - c0], F32, name="sm")
+            for e in range(2):
+                nc.vector.tensor_tensor(
+                    sm[n][:, e, :], win[2 * u + e][:].indirect(n2_t[:, c0 // 16 : c1 // 16]), pa[n][:, e, :], ALU.add
+                )
+
+        def parts(n):
+            c0, c1, u = units[n]
+            return [(0, 0, P), (1, 0, P)] if c1 - c0 == HALF else [(0, 0, 64), (0, 64, P)]
+
+        def spread(n):
+            c0, c1, u = units[n]
+            w = c1 - c0
+            nb = w // P
+            dd = work.tile([P, 2, w], F32, name="dd", tag="turn%d_0" % (n % 2), bufs=1)
+            ee = work.tile([P, 2, w], F32, name="ee", tag="turn%d_1" % (n % 2), bufs=1)
+            nc.vector.scalar_tensor_tensor(dd[:], pa[n][:], 2.0, sm[n][:], ALU.mult, ALU.subtract)
+            nc.vector.scalar_tensor_tensor(ee[:], sm[n][:], 1.32, kk[:, 2 * u : 2 * u + 2, c0:c1], ALU.mult, ALU.add)
+            d_ps[n] = psum.tile([P, nb, 2, P], F32, name="d_ps", tag="turn%d" % ((n - 1) % 3))
+            for b in range(nb):
+                for e in range(2):
+                    cols = slice(c0 + b * P, c0 + (b + 1) * P)
+                    nc.tensor.matmul(d_ps[n][:, b, e, :], sm[n][:, e, b * P : (b + 1) * P], ident[:], start=True, stop=False, is_transpose=True)
+                    nc.tensor.matmul(d_ps[n][:, b, e, :], kk[:, 2 * u + e, cols], ident[:], start=False, stop=True, is_transpose=True)
+            sq = work.tile([P, 2, 2, w], F32, name="sq", bufs=1)
+            for i, (src, scale) in enumerate(((dd, s_d), (ee, s_e))):
+                for e in range(2):
+                    t = 2 * u + e
+                    nc.scalar.activation(sq[:, i, e, :], src[:, e, :], ACT.Square, scale=scale[:, t : t + 1])
+            q_ps = psum.tile([P, nb, 2, P], F32, name="q_ps", tag="turn%d" % (n % 3))
+            for e in range(2):
+                for b in range(nb):
+                    for i in range(2):
+                        nc.tensor.matmul(q_ps[:, b, e, :], sq[:, i, e, b * P : (b + 1) * P], ident[:], start=i == 0, stop=i == 1, is_transpose=True)
+            r_t[n] = []
+            for i, (b, p0, p1) in enumerate(parts(n)):
+                root = work.tile([P, p1 - p0, 2], F32, name="root", tag="turn%d_%d" % (n % 2, i), bufs=1)
+                nc.scalar.activation(
+                    root[:], q_ps[:, b, :, p0:p1].rearrange("j e p -> j p e"), ACT.Abs_reciprocal_sqrt, bias=0.25, scale=0.5
+                )
+                r_t[n].append(root)
+
+        def product(n):
+            c0, c1, u = units[n]
+            nb = (c1 - c0) // P
+            half, b0 = c0, 0
+            z_t = work.tile([P, nb, P, 2], BF16, name="z_t")
+            for i, (b, p0, p1) in enumerate(parts(n)):
+                nc.vector.tensor_tensor(
+                    z_t[:, b, p0:p1, :], d_ps[n][:, b, :, p0:p1].rearrange("j e p -> j p e"), r_t[n][i][:], ALU.mult
+                )
+            if u == 0:
+                back[half] = psum.tile([P, nb, 2, P], F32, name="back")
+            words = z_t[:].rearrange("j b p e -> j (b p e)").bitcast(F32)
+            for b in range(nb):
+                nc.tensor.transpose(back[half][:, b0 + b, u, :], words[:, b * P : (b + 1) * P], ident[:])
+            if u == 1:
+                z_i[n] = work.tile([P, 4 * (c1 - c0)], BF16, name="z_i", align_bytes=64)
+                nc.scalar.copy(
+                    z_i[n][:].bitcast(F32).rearrange("p (b j u) -> p b j u", b=nb, u=2),
+                    back[half][:, b0 : b0 + nb, :, :].rearrange("p b u j -> p b j u"),
+                )
+
+        z_c = keep.tile([P, H], U32, name="z_c", align_bytes=64)
+        z_s = keep.tile([P, H], U8, name="z_s", align_bytes=64)
+
+        def quantise(n):
+            c0, c1, u = units[n]
+            nc.vector.quantize_mx(z_c[:, c0:c1].bitcast(FP8X4), z_s[:, c0:c1], z_i[n][:])
+
+        hw = [keep.tile([P, H], F32, name="hw%d" % t) for t in range(4)]
+        ho = [keep.tile([P, H], F32, name="ho%d" % t) for t in range(4)]
+
+        def second(t, c0, c1):
+            nc.tensor.matmul_mx(
+                h_ps[t][:, c0:c1],
+                lhsT=w1_c[:, t * P : (t + 1) * P].bitcast(FP8X4),
+                lhsT_scale=w1_s[:, t * P : (t + 1) * P],
+                rhs=z_c[:, c0:c1].bitcast(FP8X4),
+                rhs_scale=z_s[:, c0:c1],
+                start=True,
+                stop=True,
+            )
+
+        def leave(t, c0, c1):
+            nc.scalar.activation(hw[t][:, c0:c1], h_ps[t][:, c0:c1], ACT.Copy, scale=0.5)
+            nc.scalar.activation(ho[t][:, c0:c1], h_ps[t][:, c0:c1], ACT.Copy, scale=0.5)
+
+        def leave_early(t, c0, c1):
+            nc.vector.tensor_scalar(hw[t][:, c0:c1], h_ps[t][:, c0:c1], 0.5, None, ALU.mult)
+            nc.vector.tensor_scalar(ho[t][:, c0:c1], h_ps[t][:, c0:c1], 0.5, None, ALU.mult)
+
+        last = len(units)
+        for n in range(last):
+            gather_first(n)
+            gather_second(n)
+            if n >= 2:
+                product(n - 2)
+            spread(n)
+            if n == 3:
+                quantise(1)
+        w1_c = work.tile([P, N], U32, name="w1_c", tag="pa", bufs=1, align_bytes=64)
+        nc.vector.quantize_mx(w1_c[:].bitcast(FP8X4), w1_s[:], w1_bf[:].rearrange("p t m j -> p (t m j)"))
+        product(4)
+        product(5)
+        quantise(3)
+        second(0, 0, 256)
+        second(0, 256, 384)
+        leave_early(0, 0, 384)
+        quantise(5)
+        second(0, 384, 512)
+        for t in range(1, 4):
+            second(t, 0, H)
+        leave(0, 384, 512)
+
+        out_v = out.rearrange("(p t) c -> p t c", t=4)
+        us = [keep.tile([P, H], F32, name="us%d" % t) for t in range(4)]
+        u2 = [keep.tile([P, H], F32, name="u2%d" % t) for t in range(4)]
+        halves = [slice(0, HALF), slice(HALF, H)]
+        lists = [n3_t[:, 0:16], n3_t[:, 16:32]]
+
+        def step_one(t):
+            for i in range(2):
+                nc.vector.tensor_tensor(us[t][:, halves[i]], hw[t][:].indirect(lists[i]), ho[t][:, halves[i]], ALU.subtract)
+                nc.scalar.activation(u2[t][:, halves[i]], us[t][:, halves[i]], ACT.Copy, scale=2.0)
+
+        def step_two(t):
+            for i in range(2):
+                res = work.tile([P, HALF], F32, name="res", bufs=8)
+                nc.vector.tensor_tensor(res[:], us[t][:].indirect(lists[i]), u2[t][:, halves[i]], ALU.subtract)
+                nc.sync.dma_start(out_v[:, t, halves[i]], res[:])
+
+        leave(1, 0, H)
+        for t in range(5):
+            if t < 4:
+                step_one(t)
+            if t + 2 < 4:
+                leave(t + 2, 0, H)
+            if t >= 1:
+                step_two(t - 1)

@@ -39,9 +39,12 @@ def tile_picked_tokstdtwice_none_p_kernel(
         xw = keep.tile([P, T], U32, name="xw", align_bytes=64)
         xs = keep.tile([P, T], U8, name="xs", align_bytes=64)
         wa_raw = [keep.tile([P, 4, c1 - c0], F32, name="wa_raw%d" % c0) for c0, c1 in WA_PARTS]
-        w1_raw = [keep.tile([P, 4, HALF], F32, name="w1_raw%d" % i) for i in range(2)]
+        w1_raw = keep.tile([P, 4, N], F32, name="w1_raw")
         ident = keep.tile([P, P], F32, name="ident")
 
+        warm = keep.tile([P, 2], F32, name="warm")
+        nc.gpsimd.memset(warm[:], 1.0)
+        nc.scalar.activation(warm[:, 1:2], warm[:, 0:1], ACT.Abs_reciprocal_sqrt)
         nc.vector.memset(xs[:].bitcast(I32), 0)
         make_identity(nc, ident[:])
         xs_in = keep.tile([P, T], U8, name="xs_in", align_bytes=64)
@@ -55,16 +58,14 @@ def tile_picked_tokstdtwice_none_p_kernel(
             nc.sync.dma_start(wa_raw[i][:], wa_v[:, :, c0:c1])
         nc.sync.dma_start(n1_t[:], n1)
         nc.sync.dma_start(n2_t[:], n2)
-        w1_v = w1.rearrange("(p j) c -> p j c", j=4)
-        for i in range(2):
-            nc.sync.dma_start(w1_raw[i][:], w1_v[:, :, i * HALF : (i + 1) * HALF])
+        nc.sync.dma_start(w1_raw[:], w1.rearrange("(p j) c -> p j c", j=4))
         nc.sync.dma_start(n3_t[:], n3)
 
         for q in range(4):
             rows = slice(32 * q, 32 * q + 4)
             nc.vector.tensor_copy(xs[rows, :].bitcast(I32), xs_in[rows, :].bitcast(I32))
         gw = keep.tile([P, 4], F32, name="gw")
-        gk = keep.tile([P, 4], F32, name="gk")
+        gk = keep.tile([P, 4], F32, name="gk", tag="gk_w1", align_bytes=64)
         gsafe = keep.tile([P, 4], F32, name="gsafe")
         s_d = keep.tile([P, 4], F32, name="s_d")
         s_e = keep.tile([P, 4], F32, name="s_e")
@@ -74,14 +75,12 @@ def tile_picked_tokstdtwice_none_p_kernel(
         nc.vector.reciprocal(s_d[:], gsafe[:])
         nc.vector.tensor_scalar(s_e[:], s_d[:], 0.375 / 1.32, None, ALU.mult)
 
-        xg_w = keep.tile([P, S], U32, name="xg_w", align_bytes=64)
         xg_s = keep.tile([P, S], U8, name="xg_s", align_bytes=64)
         xd_w = keep.tile([P, S], U32, name="xd_w", align_bytes=64)
         xd_s = keep.tile([P, S], U8, name="xd_s", align_bytes=64)
         nc.vector.tensor_copy(xg_s[:], xs[:].indirect(offs_t[:]))
-        nc.vector.tensor_copy(xg_w[:], xw[:].indirect(offs_t[:]))
-        nc.vector.tensor_copy(xd_s[:].rearrange("p (t m) -> p t m", t=4), xg_s[:].rearrange("p (m t) -> p t m", t=4))
-        nc.vector.tensor_copy(xd_w[:].rearrange("p (t m) -> p t m", t=4), xg_w[:].rearrange("p (m t) -> p t m", t=4))
+        nc.vector.tensor_copy(xd_s[:].rearrange("p (t m) -> p m t", t=4), xg_s[:].rearrange("p (m t) -> p m t", t=4))
+        nc.vector.tensor_copy(xd_w[:].rearrange("p (t m) -> p m t", t=4), xw[:].indirect(offs_t[:]))
 
         wa_c, wa_s = [], []
         for i, (c0, c1) in enumerate(WA_PARTS):
@@ -116,19 +115,20 @@ def tile_picked_tokstdtwice_none_p_kernel(
             for t in (2 * u, 2 * u + 1):
                 nc.scalar.activation(kk[:, t, :], y_ps[t][:], ACT.Copy, scale=gk[:, t : t + 1])
 
-        w1_bf = keep.tile([P, 4, P, 4], BF16, name="w1_bf", align_bytes=64)
+        w1_bf = keep.tile([P, 4, P, 4], BF16, name="w1_bf", tag="gk_w1", align_bytes=64)
         w1_s = keep.tile([P, N], U8, name="w1_s", align_bytes=64)
 
-        for i in range(2):
-            nc.vector.tensor_copy(
+
+        def group_w1(i):
+            nc.scalar.copy(
                 w1_bf[:, :, 64 * i : 64 * i + 64, :].rearrange("p t m j -> p m t j"),
-                w1_raw[i][:].rearrange("p j (m t) -> p m t j", t=4),
+                w1_raw[:, :, i * HALF : (i + 1) * HALF].rearrange("p j (m t) -> p m t j", t=4),
             )
 
         h_ps = [psum.tile([P, H], F32, name="h%d" % t, tag="big%d" % t) for t in range(4)]
 
         units = UNITS
-        pa, sm, d_ps, r_t, back, z_i = {}, {}, {}, {}, {}, {}
+        pa, sm, d_ps, r_t, back, z_i, z_t = {}, {}, {}, {}, {}, {}, {}
 
         def gather_first(n):
             c0, c1, u = units[n]
@@ -153,9 +153,11 @@ def tile_picked_tokstdtwice_none_p_kernel(
             w = c1 - c0
             nb = w // P
             dd = work.tile([P, 2, w], F32, name="dd", tag="turn%d_0" % (n % 2), bufs=1)
-            ee = work.tile([P, 2, w], F32, name="ee", tag="turn%d_1" % (n % 2), bufs=1)
-            nc.vector.scalar_tensor_tensor(dd[:], pa[n][:], 2.0, sm[n][:], ALU.mult, ALU.subtract)
-            nc.vector.scalar_tensor_tensor(ee[:], sm[n][:], 1.32, kk[:, 2 * u : 2 * u + 2, c0:c1], ALU.mult, ALU.add)
+            ee = work.tile([P, 2, w], F32, name="ee", tag="turn%d_1" % ((n - 2) % 4), bufs=1)
+            for es in ((slice(0, 1), slice(1, 2)) if n < 2 else (slice(0, 2),)):
+                ts = slice(2 * u + es.start, 2 * u + es.stop)
+                nc.vector.scalar_tensor_tensor(dd[:, es, :], pa[n][:, es, :], 2.0, sm[n][:, es, :], ALU.mult, ALU.subtract)
+                nc.vector.scalar_tensor_tensor(ee[:, es, :], sm[n][:, es, :], 1.32, kk[:, ts, c0:c1], ALU.mult, ALU.add)
             d_ps[n] = psum.tile([P, nb, 2, P], F32, name="d_ps", tag="turn%d" % ((n - 1) % 3))
             for b in range(nb):
                 for e in range(2):
@@ -174,7 +176,7 @@ def tile_picked_tokstdtwice_none_p_kernel(
                         nc.tensor.matmul(q_ps[:, b, e, :], sq[:, i, e, b * P : (b + 1) * P], ident[:], start=i == 0, stop=i == 1, is_transpose=True)
             r_t[n] = []
             for i, (b, p0, p1) in enumerate(parts(n)):
-                root = work.tile([P, p1 - p0, 2], F32, name="root", tag="turn%d_%d" % (n % 2, i), bufs=1)
+                root = work.tile([P, p1 - p0, 2], F32, name="root", tag="turn%d_%d" % (n % (2 + 2 * i), i), bufs=1)
                 nc.scalar.activation(
                     root[:], q_ps[:, b, :, p0:p1].rearrange("j e p -> j p e"), ACT.Abs_reciprocal_sqrt, bias=0.25, scale=0.5
                 )
@@ -183,15 +185,19 @@ def tile_picked_tokstdtwice_none_p_kernel(
         def product(n):
             c0, c1, u = units[n]
             nb = (c1 - c0) // P
-            half, b0 = c0, 0
-            z_t = work.tile([P, nb, P, 2], BF16, name="z_t")
+            z_t[n] = work.tile([P, nb, P, 2], BF16, name="z_t", tag="turn%d_1" % ((n - 1) % 4), bufs=1)
             for i, (b, p0, p1) in enumerate(parts(n)):
                 nc.vector.tensor_tensor(
-                    z_t[:, b, p0:p1, :], d_ps[n][:, b, :, p0:p1].rearrange("j e p -> j p e"), r_t[n][i][:], ALU.mult
+                    z_t[n][:, b, p0:p1, :], d_ps[n][:, b, :, p0:p1].rearrange("j e p -> j p e"), r_t[n][i][:], ALU.mult
                 )
+
+        def turn_back(n):
+            c0, c1, u = units[n]
+            nb = (c1 - c0) // P
+            half, b0 = c0, 0
             if u == 0:
                 back[half] = psum.tile([P, nb, 2, P], F32, name="back")
-            words = z_t[:].rearrange("j b p e -> j (b p e)").bitcast(F32)
+            words = z_t[n][:].rearrange("j b p e -> j (b p e)").bitcast(F32)
             for b in range(nb):
                 nc.tensor.transpose(back[half][:, b0 + b, u, :], words[:, b * P : (b + 1) * P], ident[:])
             if u == 1:
@@ -208,8 +214,8 @@ def tile_picked_tokstdtwice_none_p_kernel(
             c0, c1, u = units[n]
             nc.vector.quantize_mx(z_c[:, c0:c1].bitcast(FP8X4), z_s[:, c0:c1], z_i[n][:])
 
-        hw = [keep.tile([P, H], F32, name="hw%d" % t) for t in range(4)]
-        ho = [keep.tile([P, H], F32, name="ho%d" % t) for t in range(4)]
+        hw = {t: keep.tile([P, H], F32, name="hw%d" % t) for t in range(1, 4)}
+        ho = {t: keep.tile([P, H], F32, name="ho%d" % t) for t in range(1, 4)}
 
         def second(t, c0, c1):
             nc.tensor.matmul_mx(
@@ -237,15 +243,23 @@ def tile_picked_tokstdtwice_none_p_kernel(
             if n >= 2:
                 product(n - 2)
             spread(n)
+            if n >= 2:
+                turn_back(n - 2)
+            else:
+                group_w1(n)
             if n == 3:
                 quantise(1)
         w1_c = work.tile([P, N], U32, name="w1_c", tag="pa", bufs=1, align_bytes=64)
         nc.vector.quantize_mx(w1_c[:].bitcast(FP8X4), w1_s[:], w1_bf[:].rearrange("p t m j -> p (t m j)"))
         product(4)
+        turn_back(4)
         product(5)
+        turn_back(5)
         quantise(3)
-        second(0, 0, 256)
         second(0, 256, 384)
+        second(0, 0, 256)
+        hw[0] = work.tile([P, H], F32, name="hw0", tag="turn1_0", bufs=1)
+        ho[0] = work.tile([P, H], F32, name="ho0", tag="turn1_1", bufs=1)
         leave_early(0, 0, 384)
         quantise(5)
         second(0, 384, 512)
@@ -270,7 +284,9 @@ def tile_picked_tokstdtwice_none_p_kernel(
                 nc.vector.tensor_tensor(res[:], us[t][:].indirect(lists[i]), u2[t][:, halves[i]], ALU.subtract)
                 nc.sync.dma_start(out_v[:, t, halves[i]], res[:])
 
-        leave(1, 0, H)
+        nc.scalar.activation(hw[1][:], h_ps[1][:], ACT.Copy, scale=0.5)
+        for c0 in (0, HALF):
+            nc.scalar.activation(ho[1][:, c0 : c0 + HALF], h_ps[1][:, c0 : c0 + HALF], ACT.Copy, scale=0.5)
         for t in range(5):
             if t < 4:
                 step_one(t)

@@ -1,3 +1,4 @@
+import math
 from contextlib import ExitStack
 
 import concourse.mybir as mybir
@@ -16,10 +17,20 @@ ACT = mybir.ActivationFunctionType
 P = 128
 K, T, S, N, H = 512, 2048, 512, 512, 512
 FLOPS = 2 * S * K * H + 2 * N * S * H
+HALF = H // 2
+PLANES = 4
+LIST_STEP = 16
+
 C = 0.3125
-UNITS = [(0, 256, 0), (0, 256, 1), (256, 384, 0), (256, 384, 1), (384, 512, 0), (384, 512, 1)]
-HALF = 256
+SHIFT = C / (1.0 - 2.0 * C)
+NORM2 = (1.0 - C) ** 2 + C**2
+CROSS = 2.0 * C * (1.0 - C) / NORM2
+REST = (1.0 - C - 2.0 * C * SHIFT) / (C * SHIFT)
+
 WA_PARTS = [(0, 256), (256, 384), (384, 512)]
+W1_PARTS = [(0, 192), (192, 512)]
+UNITS = [(0, 256, 0), (256, 512, 0), (0, 256, 1), (256, 384, 1), (384, 512, 1)]
+CHUNKS = [(c0, c1) for c0, c1, pair in UNITS if pair == 1]
 
 
 def tile_picked_tokstdtwice_none_p_kernel(
@@ -28,269 +39,317 @@ def tile_picked_tokstdtwice_none_p_kernel(
     nc = tc.nc
     with ExitStack() as ctx:
         keep = ctx.enter_context(tc.tile_pool(name="keep", bufs=1))
-        work = ctx.enter_context(tc.tile_pool(name="work", bufs=3))
         psum = ctx.enter_context(tc.psum_pool(name="psum", bufs=1))
 
-        def list_tile(name):
-            return keep.tile([P, 32], U16, name=name)
+        def sbuf(shape, dtype, name, slot=None, bufs=1):
+            return keep.tile(shape, dtype, name=name, tag=slot or name, bufs=bufs, align_bytes=64)
 
-        offs_t, n1_t, n2_t, n3_t = (list_tile(nm) for nm in ("offs_t", "n1_t", "n2_t", "n3_t"))
-        gt_t = keep.tile([P, 4], F32, name="gt_t")
-        xw = keep.tile([P, T], U32, name="xw", align_bytes=64)
-        xs = keep.tile([P, T], U8, name="xs", align_bytes=64)
-        wa_raw = [keep.tile([P, 4, c1 - c0], F32, name="wa_raw%d" % c0) for c0, c1 in WA_PARTS]
-        w1_raw = keep.tile([P, 4, N], F32, name="w1_raw")
-        ident = keep.tile([P, P], F32, name="ident")
+        def bank(shape, name, number):
+            return psum.tile(shape, F32, name=name, tag="bank%d" % number)
 
-        warm = keep.tile([P, 2], F32, name="warm")
-        nc.gpsimd.memset(warm[:], 1.0)
-        nc.scalar.activation(warm[:, 1:2], warm[:, 0:1], ACT.Abs_reciprocal_sqrt)
-        nc.vector.memset(xs[:].bitcast(I32), 0)
-        make_identity(nc, ident[:])
-        xs_in = keep.tile([P, T], U8, name="xs_in", align_bytes=64)
-        for q in range(4):
-            nc.sync.dma_start(xs_in[32 * q : 32 * q + 4, :].bitcast(I32), x_scales[0, 4 * q : 4 * q + 4, :].bitcast(I32))
-        nc.sync.dma_start(offs_t[:], offs)
-        nc.sync.dma_start(gt_t[:], gt.rearrange("(p t) o -> p (t o)", t=4))
-        nc.sync.dma_start(xw[:].bitcast(I32), x_words[0].rearrange("p n r -> p (n r)").bitcast(I32))
-        wa_v = wa.rearrange("(p j) c -> p j c", j=4)
-        for i, (c0, c1) in enumerate(WA_PARTS):
-            nc.sync.dma_start(wa_raw[i][:], wa_v[:, :, c0:c1])
-        nc.sync.dma_start(n1_t[:], n1)
-        nc.sync.dma_start(n2_t[:], n2)
-        nc.sync.dma_start(w1_raw[:], w1.rearrange("(p j) c -> p j c", j=4))
-        nc.sync.dma_start(n3_t[:], n3)
-
-        for q in range(4):
-            rows = slice(32 * q, 32 * q + 4)
-            nc.vector.tensor_copy(xs[rows, :].bitcast(I32), xs_in[rows, :].bitcast(I32))
-        gw = keep.tile([P, 4], F32, name="gw")
-        gk = keep.tile([P, 4], F32, name="gk", tag="gk_w1", align_bytes=64)
-        gsafe = keep.tile([P, 4], F32, name="gsafe")
-        s_d = keep.tile([P, 4], F32, name="s_d")
-        s_e = keep.tile([P, 4], F32, name="s_e")
-        nc.vector.tensor_scalar(gw[:], gt_t[:], -C, None, ALU.mult)
-        nc.vector.tensor_scalar(gk[:], gt_t[:], 1.0 - C, None, ALU.mult)
-        nc.vector.scalar_tensor_tensor(gsafe[:], gw[:], 0.0, gw[:], ALU.is_equal, ALU.add)
-        nc.vector.reciprocal(s_d[:], gsafe[:])
-        nc.vector.tensor_scalar(s_e[:], s_d[:], 0.375 / 1.32, None, ALU.mult)
-
-        xg_s = keep.tile([P, S], U8, name="xg_s", align_bytes=64)
-        xd_w = keep.tile([P, S], U32, name="xd_w", align_bytes=64)
-        xd_s = keep.tile([P, S], U8, name="xd_s", align_bytes=64)
-        nc.vector.tensor_copy(xg_s[:], xs[:].indirect(offs_t[:]))
-        nc.vector.tensor_copy(xd_s[:].rearrange("p (t m) -> p m t", t=4), xg_s[:].rearrange("p (m t) -> p m t", t=4))
-        nc.vector.tensor_copy(xd_w[:].rearrange("p (t m) -> p m t", t=4), xw[:].indirect(offs_t[:]))
-
-        wa_c, wa_s = [], []
-        for i, (c0, c1) in enumerate(WA_PARTS):
-            grouped = keep.tile([P, c1 - c0, 4], BF16, name="wa_bf%d" % i, align_bytes=64)
-            if i == 0:
-                nc.scalar.copy(grouped[:], wa_raw[i][:].rearrange("p j c -> p c j"))
-            else:
-                nc.vector.tensor_copy(grouped[:], wa_raw[i][:].rearrange("p j c -> p c j"))
-            codes = keep.tile([P, c1 - c0], U32, name="wa_c%d" % i, align_bytes=64)
-            scales = keep.tile([P, c1 - c0], U8, name="wa_s%d" % i, align_bytes=64)
-            nc.vector.quantize_mx(codes[:].bitcast(FP8X4), scales[:], grouped[:].rearrange("p c j -> p (c j)"))
-            wa_c.append(codes)
-            wa_s.append(scales)
-
-        y_ps = [psum.tile([P, H], F32, name="y%d" % t, tag="big%d" % t) for t in range(4)]
-        for t in range(4):
-            for i, (c0, c1) in enumerate(WA_PARTS):
-                nc.tensor.matmul_mx(
-                    y_ps[t][:, c0:c1],
-                    lhsT=xd_w[:, t * P : (t + 1) * P].bitcast(FP8X4),
-                    lhsT_scale=xd_s[:, t * P : (t + 1) * P],
-                    rhs=wa_c[i][:].bitcast(FP8X4),
-                    rhs_scale=wa_s[i][:],
-                    start=True,
-                    stop=True,
-                )
-        win = [keep.tile([P, H], F32, name="win%d" % t) for t in range(4)]
-        kk = keep.tile([P, 4, H], F32, name="kk")
-        for u in range(2):
-            for t in (2 * u, 2 * u + 1):
-                nc.scalar.activation(win[t][:], y_ps[t][:], ACT.Copy, scale=gw[:, t : t + 1])
-            for t in (2 * u, 2 * u + 1):
-                nc.scalar.activation(kk[:, t, :], y_ps[t][:], ACT.Copy, scale=gk[:, t : t + 1])
-
-        w1_bf = keep.tile([P, 4, P, 4], BF16, name="w1_bf", tag="gk_w1", align_bytes=64)
-        w1_s = keep.tile([P, N], U8, name="w1_s", align_bytes=64)
-
-
-        def group_w1(i):
-            nc.scalar.copy(
-                w1_bf[:, :, 64 * i : 64 * i + 64, :].rearrange("p t m j -> p m t j"),
-                w1_raw[:, :, i * HALF : (i + 1) * HALF].rearrange("p j (m t) -> p m t j", t=4),
-            )
-
-        h_ps = [psum.tile([P, H], F32, name="h%d" % t, tag="big%d" % t) for t in range(4)]
-
-        units = UNITS
-        pa, sm, d_ps, r_t, back, z_i, z_t = {}, {}, {}, {}, {}, {}, {}
-
-        def gather_first(n):
-            c0, c1, u = units[n]
-            pa[n] = work.tile([P, 2, c1 - c0], F32, name="pa", bufs=1, align_bytes=64)
-            for e in range(2):
-                nc.vector.tensor_copy(pa[n][:, e, :], win[2 * u + e][:].indirect(n1_t[:, c0 // 16 : c1 // 16]))
-
-        def gather_second(n):
-            c0, c1, u = units[n]
-            sm[n] = work.tile([P, 2, c1 - c0], F32, name="sm")
-            for e in range(2):
-                nc.vector.tensor_tensor(
-                    sm[n][:, e, :], win[2 * u + e][:].indirect(n2_t[:, c0 // 16 : c1 // 16]), pa[n][:, e, :], ALU.add
-                )
-
-        def parts(n):
-            c0, c1, u = units[n]
-            return [(0, 0, P), (1, 0, P)] if c1 - c0 == HALF else [(0, 0, 64), (0, 64, P)]
-
-        def spread(n):
-            c0, c1, u = units[n]
-            w = c1 - c0
-            nb = w // P
-            dd = work.tile([P, 2, w], F32, name="dd", tag="turn%d_0" % (n % 2), bufs=1)
-            ee = work.tile([P, 2, w], F32, name="ee", tag="turn%d_1" % ((n - 2) % 4), bufs=1)
-            for es in ((slice(0, 1), slice(1, 2)) if n < 2 else (slice(0, 2),)):
-                ts = slice(2 * u + es.start, 2 * u + es.stop)
-                nc.vector.scalar_tensor_tensor(dd[:, es, :], pa[n][:, es, :], 2.0, sm[n][:, es, :], ALU.mult, ALU.subtract)
-                nc.vector.scalar_tensor_tensor(ee[:, es, :], sm[n][:, es, :], 1.32, kk[:, ts, c0:c1], ALU.mult, ALU.add)
-            d_ps[n] = psum.tile([P, nb, 2, P], F32, name="d_ps", tag="turn%d" % ((n - 1) % 3))
-            for b in range(nb):
-                for e in range(2):
-                    cols = slice(c0 + b * P, c0 + (b + 1) * P)
-                    nc.tensor.matmul(d_ps[n][:, b, e, :], sm[n][:, e, b * P : (b + 1) * P], ident[:], start=True, stop=False, is_transpose=True)
-                    nc.tensor.matmul(d_ps[n][:, b, e, :], kk[:, 2 * u + e, cols], ident[:], start=False, stop=True, is_transpose=True)
-            sq = work.tile([P, 2, 2, w], F32, name="sq", bufs=1)
-            for i, (src, scale) in enumerate(((dd, s_d), (ee, s_e))):
-                for e in range(2):
-                    t = 2 * u + e
-                    nc.scalar.activation(sq[:, i, e, :], src[:, e, :], ACT.Square, scale=scale[:, t : t + 1])
-            q_ps = psum.tile([P, nb, 2, P], F32, name="q_ps", tag="turn%d" % (n % 3))
-            for e in range(2):
-                for b in range(nb):
-                    for i in range(2):
-                        nc.tensor.matmul(q_ps[:, b, e, :], sq[:, i, e, b * P : (b + 1) * P], ident[:], start=i == 0, stop=i == 1, is_transpose=True)
-            r_t[n] = []
-            for i, (b, p0, p1) in enumerate(parts(n)):
-                root = work.tile([P, p1 - p0, 2], F32, name="root", tag="turn%d_%d" % (n % (2 + 2 * i), i), bufs=1)
-                nc.scalar.activation(
-                    root[:], q_ps[:, b, :, p0:p1].rearrange("j e p -> j p e"), ACT.Abs_reciprocal_sqrt, bias=0.25, scale=0.5
-                )
-                r_t[n].append(root)
-
-        def product(n):
-            c0, c1, u = units[n]
-            nb = (c1 - c0) // P
-            z_t[n] = work.tile([P, nb, P, 2], BF16, name="z_t", tag="turn%d_1" % ((n - 1) % 4), bufs=1)
-            for i, (b, p0, p1) in enumerate(parts(n)):
-                nc.vector.tensor_tensor(
-                    z_t[n][:, b, p0:p1, :], d_ps[n][:, b, :, p0:p1].rearrange("j e p -> j p e"), r_t[n][i][:], ALU.mult
-                )
-
-        def turn_back(n):
-            c0, c1, u = units[n]
-            nb = (c1 - c0) // P
-            half, b0 = c0, 0
-            if u == 0:
-                back[half] = psum.tile([P, nb, 2, P], F32, name="back")
-            words = z_t[n][:].rearrange("j b p e -> j (b p e)").bitcast(F32)
-            for b in range(nb):
-                nc.tensor.transpose(back[half][:, b0 + b, u, :], words[:, b * P : (b + 1) * P], ident[:])
-            if u == 1:
-                z_i[n] = work.tile([P, 4 * (c1 - c0)], BF16, name="z_i", align_bytes=64)
-                nc.scalar.copy(
-                    z_i[n][:].bitcast(F32).rearrange("p (b j u) -> p b j u", b=nb, u=2),
-                    back[half][:, b0 : b0 + nb, :, :].rearrange("p b u j -> p b j u"),
-                )
-
-        z_c = keep.tile([P, H], U32, name="z_c", align_bytes=64)
-        z_s = keep.tile([P, H], U8, name="z_s", align_bytes=64)
-
-        def quantise(n):
-            c0, c1, u = units[n]
-            nc.vector.quantize_mx(z_c[:, c0:c1].bitcast(FP8X4), z_s[:, c0:c1], z_i[n][:])
-
-        hw = {t: keep.tile([P, H], F32, name="hw%d" % t) for t in range(1, 4)}
-        ho = {t: keep.tile([P, H], F32, name="ho%d" % t) for t in range(1, 4)}
-
-        def second(t, c0, c1):
+        def mx_product(dst, lhs_codes, lhs_scales, rhs_codes, rhs_scales):
             nc.tensor.matmul_mx(
-                h_ps[t][:, c0:c1],
-                lhsT=w1_c[:, t * P : (t + 1) * P].bitcast(FP8X4),
-                lhsT_scale=w1_s[:, t * P : (t + 1) * P],
-                rhs=z_c[:, c0:c1].bitcast(FP8X4),
-                rhs_scale=z_s[:, c0:c1],
+                dst,
+                lhsT=lhs_codes.bitcast(FP8X4),
+                lhsT_scale=lhs_scales,
+                rhs=rhs_codes.bitcast(FP8X4),
+                rhs_scale=rhs_scales,
                 start=True,
                 stop=True,
             )
 
-        def leave(t, c0, c1):
-            nc.scalar.activation(hw[t][:, c0:c1], h_ps[t][:, c0:c1], ACT.Copy, scale=0.5)
-            nc.scalar.activation(ho[t][:, c0:c1], h_ps[t][:, c0:c1], ACT.Copy, scale=0.5)
+        def add_turned(dst, terms):
+            for i, term in enumerate(terms):
+                nc.tensor.matmul(dst, term, ident[:], start=i == 0, stop=i == len(terms) - 1, is_transpose=True)
 
-        def leave_early(t, c0, c1):
-            nc.vector.tensor_scalar(hw[t][:, c0:c1], h_ps[t][:, c0:c1], 0.5, None, ALU.mult)
-            nc.vector.tensor_scalar(ho[t][:, c0:c1], h_ps[t][:, c0:c1], 0.5, None, ALU.mult)
+        def entries(list_tile, c0, c1):
+            return list_tile[:, c0 // LIST_STEP : c1 // LIST_STEP]
 
-        last = len(units)
-        for n in range(last):
-            gather_first(n)
-            gather_second(n)
-            if n >= 2:
-                product(n - 2)
-            spread(n)
-            if n >= 2:
-                turn_back(n - 2)
+        offs_t, n1_t, n2_t, n3_t = (keep.tile([P, S // LIST_STEP], U16, name=nm) for nm in ("offs_t", "n1_t", "n2_t", "n3_t"))
+        gt_t = keep.tile([P, PLANES], F32, name="gt_t")
+        xw = sbuf([P, T], U32, "xw")
+        xs = sbuf([P, T], U8, "xs")
+        wa_raw = [keep.tile([P, 4, c1 - c0], F32, name="wa_raw%d" % c0, tag="raw%d" % c0) for c0, c1 in WA_PARTS]
+        ident = keep.tile([P, P], F32, name="ident")
+
+        nc.gpsimd.memset(xs[:].bitcast(I32), 0)
+        warm = keep.tile([P, 2], F32, name="warm")
+        nc.vector.memset(warm[:], 1.0)
+        nc.scalar.activation(warm[:, 1:2], warm[:, 0:1], ACT.Abs_reciprocal_sqrt)
+        make_identity(nc, ident[:])
+        for q in range(4):
+            nc.sync.dma_start(xs[32 * q : 32 * q + 4, :].bitcast(I32), x_scales[0, 4 * q : 4 * q + 4, :].bitcast(I32))
+        nc.sync.dma_start(offs_t[:], offs)
+        nc.sync.dma_start(gt_t[:], gt.rearrange("(p t) o -> p (t o)", t=PLANES))
+        nc.sync.dma_start(xw[:].bitcast(I32), x_words[0].rearrange("p n r -> p (n r)").bitcast(I32))
+        wa_rows = wa.rearrange("(p j) c -> p j c", j=4)
+        for raw, (c0, c1) in zip(wa_raw, WA_PARTS):
+            nc.sync.dma_start(raw[:], wa_rows[:, :, c0:c1])
+        nc.sync.dma_start(n1_t[:], n1)
+        nc.sync.dma_start(n2_t[:], n2)
+        nc.sync.dma_start(n3_t[:], n3)
+        w1_rows = w1.rearrange("(p j) c -> p j c", j=4)
+        w1_raw = {}
+
+        def load_w1(i, slot):
+            c0, c1 = W1_PARTS[i]
+            w1_raw[i] = keep.tile([P, 4, c1 - c0], F32, name="w1_raw%d" % i, tag=slot)
+            nc.sync.dma_start(w1_raw[i][:], w1_rows[:, :, c0:c1])
+
+        load_w1(0, "w1_first")
+
+        g_win, g_shift, g_safe, g_inv, s_a, s_c = (
+            keep.tile([P, PLANES], F32, name=nm) for nm in ("g_win", "g_shift", "g_safe", "g_inv", "s_a", "s_c")
+        )
+        nc.vector.tensor_scalar(g_win[:], gt_t[:], -C, None, ALU.mult)
+        nc.vector.tensor_scalar(g_shift[:], gt_t[:], C * SHIFT, None, ALU.mult)
+        nc.vector.scalar_tensor_tensor(g_safe[:], g_win[:], 0.0, g_win[:], ALU.is_equal, ALU.add)
+        nc.vector.reciprocal(g_inv[:], g_safe[:])
+        nc.vector.tensor_scalar(s_a[:], g_inv[:], (1.0 - 2.0 * C) / math.sqrt(NORM2), None, ALU.mult)
+        nc.vector.tensor_scalar(s_c[:], g_inv[:], math.sqrt(NORM2), None, ALU.mult)
+
+        xg_s = sbuf([P, S], U8, "xg_s")
+        xd_w = sbuf([P, S], U32, "xd_w")
+        xd_s = sbuf([P, S], U8, "xd_s")
+        nc.vector.tensor_copy(xg_s[:], xs[:].indirect(offs_t[:]))
+        nc.vector.tensor_copy(
+            xd_s[:].rearrange("p (t m) -> p m t", t=PLANES), xg_s[:].rearrange("p (m t) -> p m t", t=PLANES)
+        )
+        nc.vector.tensor_copy(xd_w[:].rearrange("p (t m) -> p m t", t=PLANES), xw[:].indirect(offs_t[:]))
+
+        wa_c, wa_s = [], []
+        for i, (c0, c1) in enumerate(WA_PARTS):
+            grouped = sbuf([P, c1 - c0, 4], BF16, "wa_bf%d" % i)
+            dst = grouped[:].rearrange("p (c i) j -> p c j i", i=4)
+            rows = wa_raw[i][:].rearrange("p j (c i) -> p c j i", i=4)
+            if i == 0:
+                nc.scalar.copy(dst, rows)
             else:
-                group_w1(n)
-            if n == 3:
-                quantise(1)
-        w1_c = work.tile([P, N], U32, name="w1_c", tag="pa", bufs=1, align_bytes=64)
+                nc.vector.tensor_copy(dst, rows)
+            codes = sbuf([P, c1 - c0], U32, "wa_c%d" % i)
+            scales = sbuf([P, c1 - c0], U8, "wa_s%d" % i)
+            nc.vector.quantize_mx(codes[:].bitcast(FP8X4), scales[:], grouped[:].rearrange("p c j -> p (c j)"))
+            wa_c.append(codes)
+            wa_s.append(scales)
+        w1_raw_slot = "raw%d" % WA_PARTS[0][0]
+        load_w1(1, w1_raw_slot)
+
+        y_ps = [bank([P, H], "y%d" % t, t) for t in range(PLANES)]
+        y0_hi = bank([P, H], "y0_hi", 4)
+        for t in range(PLANES):
+            tokens = slice(t * P, (t + 1) * P)
+            for i, (c0, c1) in enumerate(WA_PARTS):
+                dst = y0_hi if t == 0 and c0 >= HALF else y_ps[t]
+                mx_product(dst[:, c0:c1], xd_w[:, tokens], xd_s[:, tokens], wa_c[i][:], wa_s[i][:])
+
+        win = [sbuf([P, H], F32, "win%d" % t) for t in range(PLANES)]
+        shift = [sbuf([P, 2, H], F32, "shift%d" % pair) for pair in range(2)]
+
+        def window(t):
+            nc.scalar.activation(win[t][:], y_ps[t][:], ACT.Copy, scale=g_win[:, t : t + 1])
+
+        def shift_half(t, half):
+            cols = slice(half * HALF, (half + 1) * HALF)
+            src = y0_hi if t == 0 and half == 1 else y_ps[t]
+            nc.scalar.activation(shift[t // 2][:, t % 2, cols], src[:, cols], ACT.Copy, scale=g_shift[:, t : t + 1])
+
+        ga, gb, gc, rest, sq_a, sq_c, q_ps, d_ps, root, z_t, back, z_i = ({} for i in range(12))
+        last = len(UNITS) - 1
+
+        def gathers(n):
+            c0, c1, pair = UNITS[n]
+            ga[n], gb[n], gc[n] = (sbuf([P, 2, c1 - c0], F32, "%s%d" % (nm, n)) for nm in ("ga", "gb", "gc"))
+            by_plane = n in (0, last)
+            for i, e in [(0, 0), (1, 0), (0, 1), (1, 1)] if by_plane else [(0, 0), (0, 1), (1, 0), (1, 1)]:
+                dst, list_tile = ((ga[n], n1_t), (gb[n], n2_t))[i]
+                looked_up = win[2 * pair + e][:].indirect(entries(list_tile, c0, c1))
+                nc.vector.tensor_tensor(dst[:, e, :], looked_up, shift[pair][:, e, c0:c1], ALU.add)
+            for es in (slice(0, 1), slice(1, 2)) if n == last else (slice(0, 2),):
+                nc.vector.scalar_tensor_tensor(gc[n][:, es, :], ga[n][:, es, :], -CROSS, gb[n][:, es, :], ALU.mult, ALU.add)
+
+        def squares(n, dst, src, scale, name, bufs):
+            c0, c1, pair = UNITS[n]
+            dst[n] = sbuf([P, 2, c1 - c0], F32, name, bufs=bufs)
+            for e in range(2):
+                t = 2 * pair + e
+                nc.scalar.activation(dst[n][:, e, :], src[n][:, e, :], ACT.Square, scale=scale[:, t : t + 1])
+
+        def rest_term(n):
+            c0, c1, pair = UNITS[n]
+            rest[n] = sbuf([P, 2, c1 - c0], F32, "rest%d" % n, slot="gc%d" % (n - 1))
+            nc.scalar.activation(rest[n][:], shift[pair][:, :, c0:c1], ACT.Copy, scale=REST)
+
+        def blocks(n):
+            c0, c1, pair = UNITS[n]
+            return [(b, e, slice(b * P, (b + 1) * P)) for e in range(2) for b in range((c1 - c0) // P)]
+
+        def square_sum(n):
+            c0, c1, pair = UNITS[n]
+            q_ps[n] = bank([P, (c1 - c0) // P, 2, P], "q_ps", 5 + n % 2)
+            for b, e, cols in blocks(n):
+                add_turned(q_ps[n][:, b, e, :], (sq_a[n][:, e, cols], sq_c[n][:, e, cols]))
+
+        def numerator(n, dst):
+            d_ps[n] = dst
+            for b, e, cols in blocks(n):
+                terms = (rest[n][:, e, cols], ga[n][:, e, cols], gb[n][:, e, cols])
+                add_turned(dst[:, b, e, :], terms[1:] + terms[:1] if n == 0 else terms)
+
+        def row_parts(n):
+            return [slice(0, P // 2), slice(P // 2, P)] if n == last else [slice(0, P)]
+
+        def roots(n):
+            c0, c1, pair = UNITS[n]
+            root[n] = sbuf([P, (c1 - c0) // P, P, 2], F32, "root%d" % n)
+            for ps in row_parts(n):
+                nc.scalar.activation(
+                    root[n][:, :, ps, :],
+                    q_ps[n][:, :, :, ps].rearrange("j b e p -> j b p e"),
+                    ACT.Abs_reciprocal_sqrt,
+                    bias=0.25,
+                )
+
+        def product(n, slot=None):
+            c0, c1, pair = UNITS[n]
+            z_t[n] = sbuf([P, (c1 - c0) // P, P, 2], BF16, "z_t%d" % n, slot=slot)
+            for ps in row_parts(n):
+                nc.vector.tensor_tensor(
+                    z_t[n][:, :, ps, :],
+                    d_ps[n][:, :, :, ps].rearrange("j b e p -> j b p e"),
+                    root[n][:, :, ps, :],
+                    ALU.mult,
+                )
+
+        def turn_back(n, k):
+            c0, c1, pair = UNITS[n]
+            k0, k1 = CHUNKS[k]
+            words = z_t[n][:].rearrange("j b p e -> j (b p e)").bitcast(F32)
+            for b in range((k1 - k0) // P):
+                w0 = k0 - c0 + b * P
+                nc.tensor.transpose(back[k][:, b, pair, :], words[:, w0 : w0 + P], ident[:])
+
+        def weave(k):
+            k0, k1 = CHUNKS[k]
+            z_i[k] = sbuf([P, 4 * (k1 - k0)], BF16, "z_i%d" % k)
+            nc.scalar.copy(
+                z_i[k][:].bitcast(F32).rearrange("p (b j u) -> p b j u", j=P, u=2),
+                back[k][:].rearrange("p b u j -> p b j u"),
+            )
+
+        w1_bf = sbuf([P, PLANES, P, 4], BF16, "w1_bf")
+
+        def group_w1(i):
+            c0, c1 = W1_PARTS[i]
+            nc.vector.tensor_copy(
+                w1_bf[:, :, c0 // PLANES : c1 // PLANES, :].rearrange("p t m j -> p m j t"),
+                w1_raw[i][:].rearrange("p j (m t) -> p m j t", t=PLANES),
+            )
+
+        nc.scalar.activation(win[0][:, :HALF], y_ps[0][:, :HALF], ACT.Copy, scale=g_win[:, 0:1])
+        nc.vector.tensor_scalar(win[0][:, HALF:], y0_hi[:, HALF:], g_win[:, 0:1], None, ALU.mult)
+        shift_half(0, 0)
+        window(1)
+        shift_half(1, 0)
+        group_w1(0)
+        rest_term(0)
+        shift_half(0, 1)
+        shift_half(1, 1)
+        narrow = {}
+        for n in range(len(UNITS)):
+            gathers(n)
+            squares(n, sq_a, ga, s_a, "sq_a", 2)
+            if n == 0:
+                for t in (2, 3):
+                    window(t)
+                    shift_half(t, 0)
+            squares(n, sq_c, gc, s_c, "sq_c", 1)
+            square_sum(n)
+            if n < last - 1:
+                numerator(n, bank([P, 2, 2, P], "d_ps", (7, 4, 0)[n])[:])
+            else:
+                if n == last - 1:
+                    narrow = bank([P, 2, 2, P], "d_ps", 1)
+                numerator(n, narrow[:, n - (last - 1) : n - (last - 1) + 1, :, :])
+            if n < last:
+                rest_term(n + 1)
+            if n == 0:
+                for t in (2, 3):
+                    shift_half(t, 1)
+            roots(n)
+            if n == 1:
+                group_w1(1)
+
+        for k, number in enumerate((2, 3)):
+            back[k] = bank([P, (CHUNKS[k][1] - CHUNKS[k][0]) // P, 2, P], "back", number)
+        product(0, slot="gb%d" % (last - 1))
+        product(2, slot="ga%d" % (last - 1))
+        turn_back(0, 0)
+        turn_back(2, 0)
+        weave(0)
+        product(1, slot="gc%d" % (last - 1))
+        w1_c = sbuf([P, N], U32, "w1_c", slot="win%d" % (PLANES - 1))
+        w1_s = sbuf([P, N], U8, "w1_s")
         nc.vector.quantize_mx(w1_c[:].bitcast(FP8X4), w1_s[:], w1_bf[:].rearrange("p t m j -> p (t m j)"))
+        product(3)
         product(4)
-        turn_back(4)
-        product(5)
-        turn_back(5)
-        quantise(3)
-        second(0, 256, 384)
-        second(0, 0, 256)
-        hw[0] = work.tile([P, H], F32, name="hw0", tag="turn1_0", bufs=1)
-        ho[0] = work.tile([P, H], F32, name="ho0", tag="turn1_1", bufs=1)
-        leave_early(0, 0, 384)
-        quantise(5)
-        second(0, 384, 512)
-        for t in range(1, 4):
-            second(t, 0, H)
-        leave(0, 384, 512)
+        back[2] = bank([P, 1, 2, P], "back", 5 + last % 2)
+        for k in (1, 2):
+            turn_back(1, k)
+            turn_back(2 + k, k)
+            weave(k)
 
-        out_v = out.rearrange("(p t) c -> p t c", t=4)
-        us = [keep.tile([P, H], F32, name="us%d" % t) for t in range(4)]
-        u2 = [keep.tile([P, H], F32, name="u2%d" % t) for t in range(4)]
-        halves = [slice(0, HALF), slice(HALF, H)]
-        lists = [n3_t[:, 0:16], n3_t[:, 16:32]]
+        z_c = sbuf([P, H], U32, "z_c")
+        z_s = sbuf([P, H], U8, "z_s")
+        h0_ps = []
+        for k, number in enumerate((7, 4, 5 + (last - 1) % 2)):
+            c0, c1 = CHUNKS[k]
+            nc.vector.quantize_mx(z_c[:, c0:c1].bitcast(FP8X4), z_s[:, c0:c1], z_i[k][:])
+            h0_ps.append(bank([P, c1 - c0], "h0", number))
+            mx_product(h0_ps[k][:], w1_c[:, :P], w1_s[:, :P], z_c[:, c0:c1], z_s[:, c0:c1])
+        h_ps = {}
+        for t in range(1, PLANES):
+            rows = slice(t * P, (t + 1) * P)
+            h_ps[t] = bank([P, H], "h", t - 1)
+            mx_product(h_ps[t][:], w1_c[:, rows], w1_s[:, rows], z_c[:], z_s[:])
 
-        def step_one(t):
-            for i in range(2):
-                nc.vector.tensor_tensor(us[t][:, halves[i]], hw[t][:].indirect(lists[i]), ho[t][:, halves[i]], ALU.subtract)
-                nc.scalar.activation(u2[t][:, halves[i]], us[t][:, halves[i]], ACT.Copy, scale=2.0)
+        order = [("h", 0), ("h", 1), ("u", 0), ("h", 2), ("u", 1), ("h", 3), ("u", 2), ("u", 3)]
+        windows, plain = {}, {}
+        for i, step in enumerate(order):
+            wide = 0 < i < len(order) - 1
+            windows[step] = sbuf([P, 2 * H if wide else H], F32, "window_%s%d" % step)
+            if wide:
+                plain[order[i - 1]] = windows[step][:, H:]
+        for step in order[-2:]:
+            plain[step] = sbuf([P, H], F32, "plain_%s%d" % step)[:]
+        pieces = {step: [(0, H)] for step in order}
+        pieces[order[0]] = [(0, HALF), (HALF, H)]
+        pieces[order[-1]] = CHUNKS
 
-        def step_two(t):
-            for i in range(2):
-                res = work.tile([P, HALF], F32, name="res", bufs=8)
-                nc.vector.tensor_tensor(res[:], us[t][:].indirect(lists[i]), u2[t][:, halves[i]], ALU.subtract)
-                nc.sync.dma_start(out_v[:, t, halves[i]], res[:])
+        def halve(t):
+            for dst in (windows["h", t][:, :H], plain["h", t]):
+                nc.scalar.activation(dst, h_ps[t][:], ACT.Copy, scale=0.5)
 
-        nc.scalar.activation(hw[1][:], h_ps[1][:], ACT.Copy, scale=0.5)
-        for c0 in (0, HALF):
-            nc.scalar.activation(ho[1][:, c0 : c0 + HALF], h_ps[1][:, c0 : c0 + HALF], ACT.Copy, scale=0.5)
-        for t in range(5):
-            if t < 4:
-                step_one(t)
-            if t + 2 < 4:
-                leave(t + 2, 0, H)
-            if t >= 1:
-                step_two(t - 1)
+        def look_up(step, dst, c0, c1):
+            looked_up = windows[step][:].indirect(entries(n3_t, c0, c1))
+            nc.vector.tensor_tensor(dst[:, c0:c1], looked_up, plain[step][:, c0:c1], ALU.subtract)
+
+        for dst in (windows["h", 0], plain["h", 0]):
+            nc.vector.tensor_scalar(dst[:, :HALF], h0_ps[0][:], 0.5, None, ALU.mult)
+        for dst in (windows["h", 0], plain["h", 0]):
+            for k in (1, 2):
+                nc.scalar.activation(dst[:, CHUNKS[k][0] : CHUNKS[k][1]], h0_ps[k][:], ACT.Copy, scale=0.5)
+        halve(1)
+        out_rows = out.rearrange("(p t) c -> p t c", t=PLANES)
+        for step in order:
+            kind, t = step
+            if kind == "h":
+                for c0, c1 in pieces[step]:
+                    look_up(step, windows["u", t], c0, c1)
+                nc.scalar.activation(plain["u", t], windows["u", t][:, :H], ACT.Copy, scale=2.0)
+                if t + 2 < PLANES:
+                    halve(t + 2)
+            else:
+                res = sbuf([P, H], F32, "res%d" % t)
+                for c0, c1 in pieces[step]:
+                    look_up(step, res, c0, c1)
+                    nc.sync.dma_start(out_rows[:, t, c0:c1], res[:, c0:c1])

@@ -69,7 +69,7 @@ def tile_picked_tokstdtwice_none_p_kernel(
         gt_t = keep.tile([P, PLANES], F32, name="gt_t")
         xw = sbuf([P, T], U32, "xw")
         xs = sbuf([P, T], U8, "xs")
-        wa_raw = [keep.tile([P, 4, c1 - c0], F32, name="wa_raw%d" % c0, tag="raw%d" % c0) for c0, c1 in WA_PARTS]
+        wa_raw = [sbuf([P, 4, c1 - c0], F32, "wa_raw%d" % c0) for c0, c1 in WA_PARTS]
         ident = keep.tile([P, P], F32, name="ident")
 
         nc.gpsimd.memset(xs[:].bitcast(I32), 0)
@@ -91,12 +91,12 @@ def tile_picked_tokstdtwice_none_p_kernel(
         w1_rows = w1.rearrange("(p j) c -> p j c", j=4)
         w1_raw = {}
 
-        def load_w1(i, slot):
+        def load_w1(i, slot=None):
             c0, c1 = W1_PARTS[i]
-            w1_raw[i] = keep.tile([P, 4, c1 - c0], F32, name="w1_raw%d" % i, tag=slot)
+            w1_raw[i] = sbuf([P, 4, c1 - c0], F32, "w1_raw%d" % i, slot=slot)
             nc.sync.dma_start(w1_raw[i][:], w1_rows[:, :, c0:c1])
 
-        load_w1(0, "w1_first")
+        load_w1(0)
 
         g_win, g_shift, g_safe, g_inv, s_a, s_c = (
             keep.tile([P, PLANES], F32, name=nm) for nm in ("g_win", "g_shift", "g_safe", "g_inv", "s_a", "s_c")
@@ -131,8 +131,6 @@ def tile_picked_tokstdtwice_none_p_kernel(
             nc.vector.quantize_mx(codes[:].bitcast(FP8X4), scales[:], grouped[:].rearrange("p c j -> p (c j)"))
             wa_c.append(codes)
             wa_s.append(scales)
-        w1_raw_slot = "raw%d" % WA_PARTS[0][0]
-        load_w1(1, w1_raw_slot)
 
         y_ps = [bank([P, H], "y%d" % t, t) for t in range(PLANES)]
         y0_hi = bank([P, H], "y0_hi", 4)
@@ -150,8 +148,7 @@ def tile_picked_tokstdtwice_none_p_kernel(
 
         def shift_half(t, half):
             cols = slice(half * HALF, (half + 1) * HALF)
-            src = y0_hi if t == 0 and half == 1 else y_ps[t]
-            nc.scalar.activation(shift[t // 2][:, t % 2, cols], src[:, cols], ACT.Copy, scale=g_shift[:, t : t + 1])
+            nc.scalar.activation(shift[t // 2][:, t % 2, cols], y_ps[t][:, cols], ACT.Copy, scale=g_shift[:, t : t + 1])
 
         ga, gb, gc, rest, sq_a, sq_c, q_ps, d_ps, root, z_t, back, z_i = ({} for i in range(12))
         last = len(UNITS) - 1
@@ -252,8 +249,8 @@ def tile_picked_tokstdtwice_none_p_kernel(
         shift_half(1, 0)
         group_w1(0)
         rest_term(0)
-        shift_half(0, 1)
-        shift_half(1, 1)
+        for t in (0, 1):
+            nc.vector.tensor_scalar(shift[0][:, t, HALF:], win[t][:, HALF:], -SHIFT, None, ALU.mult)
         narrow = {}
         for n in range(len(UNITS)):
             gathers(n)
@@ -277,7 +274,8 @@ def tile_picked_tokstdtwice_none_p_kernel(
                     shift_half(t, 1)
             roots(n)
             if n == 1:
-                group_w1(1)
+                load_w1(1, slot="gb%d" % n)
+        group_w1(1)
 
         for k, number in enumerate((2, 3)):
             back[k] = bank([P, (CHUNKS[k][1] - CHUNKS[k][0]) // P, 2, P], "back", number)
@@ -287,11 +285,11 @@ def tile_picked_tokstdtwice_none_p_kernel(
         turn_back(2, 0)
         weave(0)
         product(1, slot="gc%d" % (last - 1))
-        w1_c = sbuf([P, N], U32, "w1_c", slot="win%d" % (PLANES - 1))
-        w1_s = sbuf([P, N], U8, "w1_s")
-        nc.vector.quantize_mx(w1_c[:].bitcast(FP8X4), w1_s[:], w1_bf[:].rearrange("p t m j -> p (t m j)"))
         product(3)
         product(4)
+        w1_c = sbuf([P, N], U32, "w1_c", slot="root%d" % last)
+        w1_s = sbuf([P, N], U8, "w1_s")
+        nc.vector.quantize_mx(w1_c[:].bitcast(FP8X4), w1_s[:], w1_bf[:].rearrange("p t m j -> p (t m j)"))
         back[2] = bank([P, 1, 2, P], "back", 5 + last % 2)
         for k in (1, 2):
             turn_back(1, k)

import math
from contextlib import ExitStack

import concourse.mybir as mybir
from concourse.masks import make_identity

F32 = mybir.dt.float32
BF16 = mybir.dt.bfloat16
I32 = mybir.dt.int32
U32 = mybir.dt.uint32
U16 = mybir.dt.uint16
U8 = mybir.dt.uint8
FP8X4 = mybir.dt.float8_e4m3fn_x4
ALU = mybir.AluOpType
ACT = mybir.ActivationFunctionType

P = 128
K, T, S, N, H = 512, 2048, 512, 512, 512
FLOPS = 2 * S * K * H + 2 * N * S * H
HALF = H // 2
PLANES = 4
LIST_STEP = 16

C = 0.3125
SHIFT = C / (1.0 - 2.0 * C)
NORM2 = (1.0 - C) ** 2 + C**2
CROSS = 2.0 * C * (1.0 - C) / NORM2
REST = (1.0 - C - 2.0 * C * SHIFT) / (C * SHIFT)

WA_PARTS = [(0, 256), (256, 384), (384, 512)]
W1_PARTS = [(0, 192), (192, 512)]
UNITS = [(0, 256, 0), (256, 512, 0), (0, 256, 1), (256, 384, 1), (384, 512, 1)]
CHUNKS = [(c0, c1) for c0, c1, pair in UNITS if pair == 1]


def tile_picked_tokstdtwice_none_p_kernel(
    tc, x_words, x_scales, wa, gt, w1, offs, n1, n2, n3, out
):
    nc = tc.nc
    with ExitStack() as ctx:
        keep = ctx.enter_context(tc.tile_pool(name="keep", bufs=1))
        psum = ctx.enter_context(tc.psum_pool(name="psum", bufs=1))

        def sbuf(shape, dtype, name, slot=None, bufs=1):
            return keep.tile(shape, dtype, name=name, tag=slot or name, bufs=bufs, align_bytes=64)

        def bank(shape, name, number):
            return psum.tile(shape, F32, name=name, tag="bank%d" % number)

        def mx_product(dst, lhs_codes, lhs_scales, rhs_codes, rhs_scales):
            nc.tensor.matmul_mx(
                dst,
                lhsT=lhs_codes.bitcast(FP8X4),
                lhsT_scale=lhs_scales,
                rhs=rhs_codes.bitcast(FP8X4),
                rhs_scale=rhs_scales,
                start=True,
                stop=True,
            )

        def add_turned(dst, terms):
            for i, term in enumerate(terms):
                nc.tensor.matmul(dst, term, ident[:], start=i == 0, stop=i == len(terms) - 1, is_transpose=True)

        def entries(list_tile, c0, c1):
            return list_tile[:, c0 // LIST_STEP : c1 // LIST_STEP]

        offs_t, n1_t, n2_t, n3_t = (keep.tile([P, S // LIST_STEP], U16, name=nm) for nm in ("offs_t", "n1_t", "n2_t", "n3_t"))
        gt_t = keep.tile([P, PLANES], F32, name="gt_t")
        xw = sbuf([P, T], U32, "xw")
        xs = sbuf([P, T], U8, "xs")
        wa_raw = [sbuf([P, 4, c1 - c0], F32, "wa_raw%d" % c0) for c0, c1 in WA_PARTS]
        ident = keep.tile([P, P], F32, name="ident")

        nc.gpsimd.memset(xs[:].bitcast(I32), 0)
        warm = keep.tile([P, 2], F32, name="warm")
        nc.vector.memset(warm[:], 1.0)
        nc.scalar.activation(warm[:, 1:2], warm[:, 0:1], ACT.Abs_reciprocal_sqrt)
        make_identity(nc, ident[:])
        for q in range(4):
            nc.sync.dma_start(xs[32 * q : 32 * q + 4, :].bitcast(I32), x_scales[0, 4 * q : 4 * q + 4, :].bitcast(I32))
        nc.sync.dma_start(offs_t[:], offs)
        nc.sync.dma_start(gt_t[:], gt.rearrange("(p t) o -> p (t o)", t=PLANES))
        nc.sync.dma_start(xw[:].bitcast(I32), x_words[0].rearrange("p n r -> p (n r)").bitcast(I32))
        wa_rows = wa.rearrange("(p j) c -> p j c", j=4)
        for raw, (c0, c1) in zip(wa_raw, WA_PARTS):
            nc.sync.dma_start(raw[:], wa_rows[:, :, c0:c1])
        nc.sync.dma_start(n1_t[:], n1)
        nc.sync.dma_start(n2_t[:], n2)
        nc.sync.dma_start(n3_t[:], n3)
        w1_rows = w1.rearrange("(p j) c -> p j c", j=4)
        w1_raw = {}

        def load_w1(i, slot=None):
            c0, c1 = W1_PARTS[i]
            w1_raw[i] = sbuf([P, 4, c1 - c0], F32, "w1_raw%d" % i, slot=slot)
            nc.sync.dma_start(w1_raw[i][:], w1_rows[:, :, c0:c1])

        load_w1(0)

        g_win, g_shift, g_safe, g_inv, s_a, s_c = (
            keep.tile([P, PLANES], F32, name=nm) for nm in ("g_win", "g_shift", "g_safe", "g_inv", "s_a", "s_c")
        )
        nc.vector.tensor_scalar(g_win[:], gt_t[:], -C, None, ALU.mult)
        nc.vector.tensor_scalar(g_shift[:], gt_t[:], C * SHIFT, None, ALU.mult)
        nc.vector.scalar_tensor_tensor(g_safe[:], g_win[:], 0.0, g_win[:], ALU.is_equal, ALU.add)
        nc.vector.reciprocal(g_inv[:], g_safe[:])
        nc.vector.tensor_scalar(s_a[:], g_inv[:], (1.0 - 2.0 * C) / math.sqrt(NORM2), None, ALU.mult)
        nc.vector.tensor_scalar(s_c[:], g_inv[:], math.sqrt(NORM2), None, ALU.mult)

        xg_s = sbuf([P, S], U8, "xg_s")
        xd_w = sbuf([P, S], U32, "xd_w")
        xd_s = sbuf([P, S], U8, "xd_s")
        nc.vector.tensor_copy(xg_s[:], xs[:].indirect(offs_t[:]))
        nc.vector.tensor_copy(
            xd_s[:].rearrange("p (t m) -> p m t", t=PLANES), xg_s[:].rearrange("p (m t) -> p m t", t=PLANES)
        )
        nc.vector.tensor_copy(xd_w[:].rearrange("p (t m) -> p m t", t=PLANES), xw[:].indirect(offs_t[:]))

        wa_c, wa_s = [], []
        for i, (c0, c1) in enumerate(WA_PARTS):
            grouped = sbuf([P, c1 - c0, 4], BF16, "wa_bf%d" % i)
            dst = grouped[:].rearrange("p (c i) j -> p c j i", i=4)
            rows = wa_raw[i][:].rearrange("p j (c i) -> p c j i", i=4)
            if i == 0:
                nc.scalar.copy(dst, rows)
            else:
                nc.vector.tensor_copy(dst, rows)
            codes = sbuf([P, c1 - c0], U32, "wa_c%d" % i)
            scales = sbuf([P, c1 - c0], U8, "wa_s%d" % i)
            nc.vector.quantize_mx(codes[:].bitcast(FP8X4), scales[:], grouped[:].rearrange("p c j -> p (c j)"))
            wa_c.append(codes)
            wa_s.append(scales)

        y_ps = [bank([P, H], "y%d" % t, t) for t in range(PLANES)]
        y0_hi = bank([P, H], "y0_hi", 4)
        for t in range(PLANES):
            tokens = slice(t * P, (t + 1) * P)
            for i, (c0, c1) in enumerate(WA_PARTS):
                dst = y0_hi if t == 0 and c0 >= HALF else y_ps[t]
                mx_product(dst[:, c0:c1], xd_w[:, tokens], xd_s[:, tokens], wa_c[i][:], wa_s[i][:])

        win = [sbuf([P, H], F32, "win%d" % t) for t in range(PLANES)]
        shift = [sbuf([P, 2, H], F32, "shift%d" % pair) for pair in range(2)]

        def window(t):
            nc.scalar.activation(win[t][:], y_ps[t][:], ACT.Copy, scale=g_win[:, t : t + 1])

        def shift_half(t, half):
            cols = slice(half * HALF, (half + 1) * HALF)
            nc.scalar.activation(shift[t // 2][:, t % 2, cols], y_ps[t][:, cols], ACT.Copy, scale=g_shift[:, t : t + 1])

        ga, gb, gc, rest, sq_a, sq_c, q_ps, d_ps, root, z_t, back, z_i = ({} for i in range(12))
        last = len(UNITS) - 1

        def gathers(n):
            c0, c1, pair = UNITS[n]
            ga[n], gb[n], gc[n] = (sbuf([P, 2, c1 - c0], F32, "%s%d" % (nm, n)) for nm in ("ga", "gb", "gc"))
            by_plane = n in (0, last)
            for i, e in [(0, 0), (1, 0), (0, 1), (1, 1)] if by_plane else [(0, 0), (0, 1), (1, 0), (1, 1)]:
                dst, list_tile = ((ga[n], n1_t), (gb[n], n2_t))[i]
                looked_up = win[2 * pair + e][:].indirect(entries(list_tile, c0, c1))
                nc.vector.tensor_tensor(dst[:, e, :], looked_up, shift[pair][:, e, c0:c1], ALU.add)
            for es in (slice(0, 1), slice(1, 2)) if n == last else (slice(0, 2),):
                nc.vector.scalar_tensor_tensor(gc[n][:, es, :], ga[n][:, es, :], -CROSS, gb[n][:, es, :], ALU.mult, ALU.add)

        def squares(n, dst, src, scale, name, bufs):
            c0, c1, pair = UNITS[n]
            dst[n] = sbuf([P, 2, c1 - c0], F32, name, bufs=bufs)
            for e in range(2):
                t = 2 * pair + e
                nc.scalar.activation(dst[n][:, e, :], src[n][:, e, :], ACT.Square, scale=scale[:, t : t + 1])

        def rest_term(n):
            c0, c1, pair = UNITS[n]
            rest[n] = sbuf([P, 2, c1 - c0], F32, "rest%d" % n, slot="gc%d" % (n - 1))
            nc.scalar.activation(rest[n][:], shift[pair][:, :, c0:c1], ACT.Copy, scale=REST)

        def blocks(n):
            c0, c1, pair = UNITS[n]
            return [(b, e, slice(b * P, (b + 1) * P)) for e in range(2) for b in range((c1 - c0) // P)]

        def square_sum(n):
            c0, c1, pair = UNITS[n]
            q_ps[n] = bank([P, (c1 - c0) // P, 2, P], "q_ps", 5 + n % 2)
            for b, e, cols in blocks(n):
                add_turned(q_ps[n][:, b, e, :], (sq_a[n][:, e, cols], sq_c[n][:, e, cols]))

        def numerator(n, dst):
            d_ps[n] = dst
            for b, e, cols in blocks(n):
                terms = (rest[n][:, e, cols], ga[n][:, e, cols], gb[n][:, e, cols])
                add_turned(dst[:, b, e, :], terms[1:] + terms[:1] if n == 0 else terms)

        def row_parts(n):
            return [slice(0, P // 2), slice(P // 2, P)] if n == last else [slice(0, P)]

        def roots(n):
            c0, c1, pair = UNITS[n]
            root[n] = sbuf([P, (c1 - c0) // P, P, 2], F32, "root%d" % n)
            for ps in row_parts(n):
                nc.scalar.activation(
                    root[n][:, :, ps, :],
                    q_ps[n][:, :, :, ps].rearrange("j b e p -> j b p e"),
                    ACT.Abs_reciprocal_sqrt,
                    bias=0.25,
                )

        def product(n, slot=None):
            c0, c1, pair = UNITS[n]
            z_t[n] = sbuf([P, (c1 - c0) // P, P, 2], BF16, "z_t%d" % n, slot=slot)
            for ps in row_parts(n):
                nc.vector.tensor_tensor(
                    z_t[n][:, :, ps, :],
                    d_ps[n][:, :, :, ps].rearrange("j b e p -> j b p e"),
                    root[n][:, :, ps, :],
                    ALU.mult,
                )

        def turn_back(n, k):
            c0, c1, pair = UNITS[n]
            k0, k1 = CHUNKS[k]
            words = z_t[n][:].rearrange("j b p e -> j (b p e)").bitcast(F32)
            for b in range((k1 - k0) // P):
                w0 = k0 - c0 + b * P
                nc.tensor.transpose(back[k][:, b, pair, :], words[:, w0 : w0 + P], ident[:])

        def weave(k):
            k0, k1 = CHUNKS[k]
            z_i[k] = sbuf([P, 4 * (k1 - k0)], BF16, "z_i%d" % k)
            nc.scalar.copy(
                z_i[k][:].bitcast(F32).rearrange("p (b j u) -> p b j u", j=P, u=2),
                back[k][:].rearrange("p b u j -> p b j u"),
            )

        w1_bf = sbuf([P, PLANES, P, 4], BF16, "w1_bf")

        def group_w1(i):
            c0, c1 = W1_PARTS[i]
            nc.vector.tensor_copy(
                w1_bf[:, :, c0 // PLANES : c1 // PLANES, :].rearrange("p t m j -> p m j t"),
                w1_raw[i][:].rearrange("p j (m t) -> p m j t", t=PLANES),
            )

        nc.scalar.activation(win[0][:, :HALF], y_ps[0][:, :HALF], ACT.Copy, scale=g_win[:, 0:1])
        nc.vector.tensor_scalar(win[0][:, HALF:], y0_hi[:, HALF:], g_win[:, 0:1], None, ALU.mult)
        shift_half(0, 0)
        window(1)
        shift_half(1, 0)
        group_w1(0)
        rest_term(0)
        for t in (0, 1):
            nc.vector.tensor_scalar(shift[0][:, t, HALF:], win[t][:, HALF:], -SHIFT, None, ALU.mult)
        narrow = {}
        for n in range(len(UNITS)):
            gathers(n)
            squares(n, sq_a, ga, s_a, "sq_a", 2)
            if n == 0:
                for t in (2, 3):
                    window(t)
                    shift_half(t, 0)
            squares(n, sq_c, gc, s_c, "sq_c", 1)
            square_sum(n)
            if n < last - 1:
                numerator(n, bank([P, 2, 2, P], "d_ps", (7, 4, 0)[n])[:])
            else:
                if n == last - 1:
                    narrow = bank([P, 2, 2, P], "d_ps", 1)
                numerator(n, narrow[:, n - (last - 1) : n - (last - 1) + 1, :, :])
            if n < last:
                rest_term(n + 1)
            if n == 0:
                for t in (2, 3):
                    shift_half(t, 1)
            roots(n)
            if n == 1:
                load_w1(1, slot="gb%d" % n)
        group_w1(1)

        for k, number in enumerate((2, 3)):
            back[k] = bank([P, (CHUNKS[k][1] - CHUNKS[k][0]) // P, 2, P], "back", number)
        product(0, slot="gb%d" % (last - 1))
        product(2, slot="ga%d" % (last - 1))
        turn_back(0, 0)
        turn_back(2, 0)
        weave(0)
        product(1, slot="gc%d" % (last - 1))
        product(3)
        product(4)
        w1_c = sbuf([P, N], U32, "w1_c", slot="root%d" % last)
        w1_s = sbuf([P, N], U8, "w1_s")
        nc.vector.quantize_mx(w1_c[:].bitcast(FP8X4), w1_s[:], w1_bf[:].rearrange("p t m j -> p (t m j)"))
        back[2] = bank([P, 1, 2, P], "back", 5 + last % 2)
        for k in (1, 2):
            turn_back(1, k)
            turn_back(2 + k, k)
            weave(k)

        z_c = sbuf([P, H], U32, "z_c")
        z_s = sbuf([P, H], U8, "z_s")
        h0_ps = []
        for k, number in enumerate((7, 4, 5 + (last - 1) % 2)):
            c0, c1 = CHUNKS[k]
            nc.vector.quantize_mx(z_c[:, c0:c1].bitcast(FP8X4), z_s[:, c0:c1], z_i[k][:])
            h0_ps.append(bank([P, c1 - c0], "h0", number))
            mx_product(h0_ps[k][:], w1_c[:, :P], w1_s[:, :P], z_c[:, c0:c1], z_s[:, c0:c1])
        h_ps = {}
        for t in range(1, PLANES):
            rows = slice(t * P, (t + 1) * P)
            h_ps[t] = bank([P, H], "h", t - 1)
            mx_product(h_ps[t][:], w1_c[:, rows], w1_s[:, rows], z_c[:], z_s[:])

        order = [("h", 0), ("h", 1), ("u", 0), ("h", 2), ("u", 1), ("h", 3), ("u", 2), ("u", 3)]
        windows, plain = {}, {}
        for i, step in enumerate(order):
            wide = 0 < i < len(order) - 1
            windows[step] = sbuf([P, 2 * H if wide else H], F32, "window_%s%d" % step)
            if wide:
                plain[order[i - 1]] = windows[step][:, H:]
        for step in order[-2:]:
            plain[step] = sbuf([P, H], F32, "plain_%s%d" % step)[:]
        pieces = {step: [(0, H)] for step in order}
        pieces[order[0]] = [(0, HALF), (HALF, H)]
        pieces[order[-1]] = CHUNKS

        def halve(t):
            for dst in (windows["h", t][:, :H], plain["h", t]):
                nc.scalar.activation(dst, h_ps[t][:], ACT.Copy, scale=0.5)

        def look_up(step, dst, c0, c1):
            looked_up = windows[step][:].indirect(entries(n3_t, c0, c1))
            nc.vector.tensor_tensor(dst[:, c0:c1], looked_up, plain[step][:, c0:c1], ALU.subtract)

        for dst in (windows["h", 0], plain["h", 0]):
            nc.vector.tensor_scalar(dst[:, :HALF], h0_ps[0][:], 0.5, None, ALU.mult)
        for dst in (windows["h", 0], plain["h", 0]):
            for k in (1, 2):
                nc.scalar.activation(dst[:, CHUNKS[k][0] : CHUNKS[k][1]], h0_ps[k][:], ACT.Copy, scale=0.5)
        halve(1)
        out_rows = out.rearrange("(p t) c -> p t c", t=PLANES)
        for step in order:
            kind, t = step
            if kind == "h":
                for c0, c1 in pieces[step]:
                    look_up(step, windows["u", t], c0, c1)
                nc.scalar.activation(plain["u", t], windows["u", t][:, :H], ACT.Copy, scale=2.0)
                if t + 2 < PLANES:
                    halve(t + 2)
            else:
                res = sbuf([P, H], F32, "res%d" % t)
                for c0, c1 in pieces[step]:
                    look_up(step, res, c0, c1)
                    nc.sync.dma_start(out_rows[:, t, c0:c1], res[:, c0:c1])
